import numpy as np
import ml_dtypes


def mxq(x, axis, fmt="e4m3"):
    dtype, down = {"e4m3": (ml_dtypes.float8_e4m3fn, 7), "e5m2": (ml_dtypes.float8_e5m2, 14)}[fmt]
    v = np.moveaxis(np.asarray(x, np.float32).astype(ml_dtypes.bfloat16).astype(np.float64), axis, -1)
    blocks = v.reshape(v.shape[:-1] + (-1, 32))
    amax = np.abs(blocks).max(-1, keepdims=True)
    byte = np.maximum(np.where(amax > 0, np.frexp(amax)[1] - 1 + 127, 0) - down, 1)
    scale = np.exp2(byte - 127.0)
    codes = (blocks / scale).astype(np.float32).astype(dtype).astype(np.float64)
    return np.moveaxis((codes * scale).reshape(v.shape), -1, axis)


WIDE = False


def mx_kscale(k):
    if not WIDE:
        return np.ones(k)
    levels = np.array([10, -10, 5, -5, 0])
    if k % 512:
        return np.exp2(np.random.permutation(np.resize(levels, k // 32))).repeat(32)
    a = np.empty((k // 512, 16))
    for p in range(k // 512):
        a[p, :8] = np.random.permutation(np.resize(levels, 8))
        for g in range(8):
            far = levels[np.abs(levels - a[p, g]) >= 10]
            a[p, g + 8] = far[np.random.randint(len(far))]
    return np.exp2(a.ravel()).repeat(32)


def f64(x):
    return np.asarray(x).astype(np.float64)


def striped(idx):
    return np.tile(idx.reshape(-1, 16).T, (8, 1)).astype(np.uint16)


def unstriped(offs):
    return offs[:16].T.reshape(-1).astype(np.int64)


def silu(v):
    return v / (1.0 + np.exp(-np.maximum(v, -700.0)))


K, T, E, C, H, N = 512, 1280, 8, 128, 512, 384


def by_expert(wq, xq):
    return np.concatenate([wq[e].T @ xq[:, e * C:(e + 1) * C] for e in range(E)], axis=1)


def setup_inputs():
    n = np.random.standard_normal
    s = mx_kscale(K)[:, None]
    u = mx_kscale(H)
    return {
        "xT": (n((K, T)) * s).astype(np.float32),
        "xr": n((N, T)).astype(np.float32),
        "w1": (n((E, K, H)) / np.sqrt(K) / s[None]).astype(np.float32),
        "w3": (n((E, K, H)) / np.sqrt(K) / s[None] * u[None, None, :]).astype(np.float32),
        "w2": (n((E, H, N)) / np.sqrt(H) / u[None, :, None]).astype(np.float32),
        "gate": np.tile(np.random.uniform(0.2, 1.0, E * C), (N, 1)).astype(np.float32),
        "offs": striped(np.random.permutation(T)[:E * C]),
    }


def reference(xT, xr, w1, w3, w2, gate, offs):
    idx = unstriped(offs)
    xq = mxq(f64(xT)[:, idx], 0, "e4m3")
    h = silu(by_expert(mxq(f64(w1), 1, "e4m3"), xq))
    h = h * by_expert(mxq(f64(w3), 1, "e4m3"), xq)
    y = by_expert(mxq(f64(w2), 1, "e4m3"), mxq(h, 0, "e4m3"))
    out = f64(xr).copy()
    out[:, idx] += f64(gate) * y
    return out

@@ -1,0 +1,196 @@
+from contextlib import ExitStack
+
+import concourse.mybir as mybir
+
+K, T, E, C, H, N = 512, 1280, 8, 128, 512, 384
+S = E * C
+P = 128
+F32 = mybir.dt.float32
+BF16 = mybir.dt.bfloat16
+U32 = mybir.dt.uint32
+U8 = mybir.dt.uint8
+U16 = mybir.dt.uint16
+FP8X4 = mybir.dt.float8_e4m3fn_x4
+COPY = mybir.ActivationFunctionType.Copy
+SILU = mybir.ActivationFunctionType.Silu
+MULT = mybir.AluOpType.mult
+ADD = mybir.AluOpType.add
+
+FLOPS = 2 * S * (2 * K * H + H * N)
+BYTES = 4 * (K * T + N * T + E * K * H * 2 + E * H * N + P * S + N * T) + 2 * P * S // 16
+
+XT_CHUNKS = ((0, 256), (256, 768), (768, 1280))
+X_ENG = ["s","s","svv"]
+UP1 = ["v","v","s","s","ssv","ssv","s","svv"]
+UP3 = ["s","s","ssv","sv","s","sv","ssv","ssv"]
+DOWN = ["s","s","ssv","ssv","s","ssv","s","s"]
+ORDER = ["b0","b2","a1","x1","x2","x0","o0","d0","A0","b1","d1","a3","b3","g0","d3","d2","b4","a4","a2","a5","b6","b5","a6","d5","d4","a7","d7","b7","d6","r1","r0","r2"]
+GATHERS = ((0, 256), (256, 1024))
+SCATTERS = {1: ((0, 256),), 3: ((256, 512),), 5: ((512, 704),), 6: ((704, 864),), 7: ((864, 1024),)}
+
+
+def tile_moe_res_glu_silu_kernel(tc, xT, xr, w1, w3, w2, gate, offs, out):
+    nc = tc.nc
+    with ExitStack() as ctx:
+        held = ctx.enter_context(tc.tile_pool(name="held", bufs=1))
+        raw = ctx.enter_context(tc.tile_pool(name="raw", bufs=8))
+        mid = ctx.enter_context(tc.tile_pool(name="mid", bufs=3))
+        cod = ctx.enter_context(tc.tile_pool(name="cod", bufs=3))
+        ps = ctx.enter_context(tc.psum_pool(name="ps", bufs=2))
+
+        offsets = held.tile([P, S // 16], U16, name="offsets")
+        gate_sb = held.tile([P, S], F32, name="gate_sb")
+        x_codes = held.tile([P, T], U32, name="x_codes", align_bytes=64)
+        x_scales = held.tile([P, T], U8, name="x_scales", align_bytes=64)
+        y_sb = held.tile([P, 3, S], F32, name="y_sb")
+        windows = [held.tile([P, T], F32, name=f"window{b}") for b in range(3)]
+        res = [held.tile([P, T], F32, name=f"res{b}") for b in range(3)]
+        g_codes = [held.tile([P, g1 - g0], U32, name=f"g_codes{g0}", align_bytes=64) for g0, g1 in GATHERS]
+        g_scales = [held.tile([P, g1 - g0], U8, name=f"g_scales{g0}", align_bytes=64) for g0, g1 in GATHERS]
+
+        x_raw = {}
+        w1_raw, w3_raw, w2_raw = {}, {}, {}
+
+        def load_x(i):
+            c0, c1 = XT_CHUNKS[i]
+            t = raw.tile([P, 4, H], F32, name="raw_up", bufs=9)
+            x_raw[i] = t
+            nc.sync.dma_start(out=t[:, :, 0 : c1 - c0], in_=xT.rearrange("(p j) t -> p j t", j=4)[:, :, c0:c1])
+
+        def load_up(dst, w, e, parts):
+            t = raw.tile([P, 4, H], F32, name="raw_up", bufs=9)
+            dst[e] = t
+            view = w[e].rearrange("(p j) i -> p j i", j=4)
+            step = H // parts
+            for q in range(parts):
+                nc.sync.dma_start(out=t[:, :, q * step : (q + 1) * step], in_=view[:, :, q * step : (q + 1) * step])
+
+        def load_down(e):
+            t = raw.tile([P, 4, N], F32, name="raw_down", bufs=4)
+            w2_raw[e] = t
+            nc.sync.dma_start(out=t[:], in_=w2[e].rearrange("(p j) n -> p j n", j=4))
+
+        for item in ORDER:
+            k, i = item[0], int(item[1:])
+            if k == "x":
+                load_x(i)
+            elif k == "a" or k == "A":
+                load_up(w1_raw, w1, i, 2 if k == "A" else 1)
+            elif k == "b" or k == "B":
+                load_up(w3_raw, w3, i, 2 if k == "B" else 1)
+            elif k == "d":
+                load_down(i)
+            elif k == "o":
+                nc.sync.dma_start(offsets[:], offs)
+            elif k == "g":
+                nc.sync.dma_start(out=gate_sb[:], in_=gate[0:P, :])
+            else:
+                nc.sync.dma_start(out=res[i][:], in_=xr[i * P : (i + 1) * P, :])
+
+        nc.gpsimd.memset(x_scales[:], 0)
+        for b in range(3):
+            nc.vector.memset(windows[b][:], 0.0)
+
+        def move(engine, dst, src):
+            if engine == "s":
+                nc.scalar.activation(out=dst, in_=src, func=COPY)
+            elif engine == "g":
+                nc.gpsimd.tensor_scalar(out=dst, in0=src, scalar1=1.0, scalar2=0.0, op0=MULT, op1=ADD)
+            else:
+                nc.vector.tensor_copy(out=dst, in_=src)
+
+        def spread(engines, dst, src, count):
+            step = count // len(engines)
+            q = 0
+            while q < len(engines):
+                r = q
+                while r < len(engines) and engines[r] == engines[q]:
+                    r += 1
+                move(engines[q], dst[:, q * step : (count if r == len(engines) else r * step)], src[:, q * step : (count if r == len(engines) else r * step)])
+                q = r
+
+        for i, (c0, c1) in enumerate(XT_CHUNKS):
+            w = c1 - c0
+            x = x_raw[i]
+            xb = mid.tile([P, 4 * H], BF16, name="bf_up", bufs=7, align_bytes=64)
+            spread(X_ENG[i], xb[:, 0 : 4 * w].rearrange("p (c i j) -> p c j i", i=4, j=4), x[:, :, 0:w].rearrange("p j (c i) -> p c j i", i=4), w // 4)
+            nc.vector.quantize_mx(out=x_codes[:, c0:c1].bitcast(FP8X4), scales=x_scales[:, c0:c1], in_=xb[:, 0 : 4 * w])
+
+        def gather(i):
+            g0, g1 = GATHERS[i]
+            cols = offsets[:, g0 // 16 : g1 // 16]
+            nc.vector.tensor_copy(out=g_codes[i][:], in_=x_codes[:].indirect(cols))
+            nc.vector.tensor_copy(out=g_scales[i][:], in_=x_scales[:].indirect(cols))
+
+        def slot_operand(e):
+            for i, (g0, g1) in enumerate(GATHERS):
+                if g0 <= e * C < g1:
+                    a = e * C - g0
+                    return g_codes[i][:, a : a + C].bitcast(FP8X4), g_scales[i][:, a : a + C]
+
+        def quantize_up(w_raw, tag, engines):
+            wb = mid.tile([P, 4 * H], BF16, name="bf_up", bufs=7, align_bytes=64)
+            dst = wb[:].rearrange("p (t m j) -> p m j t", t=4, j=4)
+            src = w_raw[:].rearrange("p j (m t) -> p m j t", t=4)
+            spread(engines, dst, src, P)
+            codes = cod.tile([P, H], U32, name=f"codes_{tag}", align_bytes=64)
+            scales = cod.tile([P, H], U8, name=f"scales_{tag}", align_bytes=64)
+            nc.vector.quantize_mx(out=codes[:].bitcast(FP8X4), scales=scales[:], in_=wb[:])
+            return codes, scales
+
+        def product(bank, codes, scales, x, blocks):
+            for t in range(blocks):
+                cols = slice(t * P, (t + 1) * P)
+                nc.tensor.matmul_mx(
+                    out=bank[:, t, :], lhsT=codes[:, cols].bitcast(FP8X4), lhsT_scale=scales[:, cols],
+                    rhs=x[0], rhs_scale=x[1], start=True, stop=True)
+
+        def down(e, h):
+            w2b = mid.tile([P, 4 * N], BF16, name="bf_down", align_bytes=64)
+            dst = w2b[:].rearrange("p (c i j) -> p c j i", i=4, j=4)
+            src = w2_raw[e][:].rearrange("p j (c i) -> p c j i", i=4)
+            spread(DOWN[e], dst, src, N // 4)
+            codes = cod.tile([P, N], U32, name="codes_down", align_bytes=64)
+            scales = cod.tile([P, N], U8, name="scales_down", align_bytes=64)
+            for c0, c1 in ((0, 256), (256, 384)):
+                nc.vector.quantize_mx(out=codes[:, c0:c1].bitcast(FP8X4), scales=scales[:, c0:c1], in_=w2b[:, 4 * c0 : 4 * c1])
+            y_ps = ps.tile([P, 3, C], F32, name="y_ps", bufs=2)
+            product(y_ps, codes, scales, h, 3)
+            nc.vector.tensor_tensor(
+                out=y_sb[:, :, e * C : (e + 1) * C], in0=y_ps[:],
+                in1=gate_sb[:, e * C : (e + 1) * C].unsqueeze(1).to_broadcast([P, 3, C]), op=MULT)
+            for s0, s1 in SCATTERS.get(e, ()):
+                cols = offsets[:, s0 // 16 : s1 // 16]
+                for b in range(3):
+                    nc.vector.tensor_copy(out=windows[b][:].indirect(cols), in_=y_sb[:, b, s0:s1])
+                    if e == E - 1:
+                        nc.vector.tensor_tensor(out=res[b][:], in0=windows[b][:], in1=res[b][:], op=ADD)
+                        nc.sync.dma_start(out=out[b * P : (b + 1) * P, :], in_=res[b][:])
+
+        prev = None
+        for e in range(E):
+            c1, s1 = quantize_up(w1_raw[e], "w1", UP1[e])
+            if e == 0:
+                gather(0)
+            c3, s3 = quantize_up(w3_raw[e], "w3", UP3[e])
+            x = slot_operand(e)
+            a_ps = ps.tile([P, 4, C], F32, name="a_ps", bufs=3)
+            b_ps = ps.tile([P, 4, C], F32, name="b_ps", bufs=3)
+            product(a_ps, c1, s1, x, 4)
+            product(b_ps, c3, s3, x, 4)
+            sil = mid.tile([P, 4, C], F32, name="sil")
+            nc.scalar.activation(out=sil[:], in_=a_ps[:], func=SILU)
+            hb = mid.tile([P, 4 * C], BF16, name="hb", align_bytes=64)
+            nc.vector.tensor_tensor(
+                out=hb[:].rearrange("p (c i j) -> p c j i", i=4, j=4),
+                in0=b_ps[:].rearrange("p j (c i) -> p c j i", i=4),
+                in1=sil[:].rearrange("p j (c i) -> p c j i", i=4), op=MULT)
+            if e == 0:
+                gather(1)
+            hc = cod.tile([P, C], U32, name="hc", align_bytes=64)
+            hs = cod.tile([P, C], U8, name="hs", align_bytes=64)
+            nc.vector.quantize_mx(out=hc[:].bitcast(FP8X4), scales=hs[:], in_=hb[:])
+            if e > 0:
+                down(e - 1, prev)
+            prev = (hc[:].bitcast(FP8X4), hs[:])
+        down(E - 1, prev)

@@ -20,22 +20,24 @@ FLOPS = 2 * S * (2 * K * H + H * N)
 BYTES = 4 * (K * T + N * T + E * K * H * 2 + E * H * N + P * S + N * T) + 2 * P * S // 16
 
 XT_CHUNKS = ((0, 256), (256, 768), (768, 1280))
-X_ENG = ["s","s","svv"]
-UP1 = ["v","v","s","s","ssv","ssv","s","svv"]
-UP3 = ["s","s","ssv","sv","s","sv","ssv","ssv"]
-DOWN = ["s","s","ssv","ssv","s","ssv","s","s"]
-ORDER = ["b0","b2","a1","x1","x2","x0","o0","d0","A0","b1","d1","a3","b3","g0","d3","d2","b4","a4","a2","a5","b6","b5","a6","d5","d4","a7","d7","b7","d6","r1","r0","r2"]
+X_ENG = ["s","ssv","sssv"]
+UP1 = ["v","sv","s","ssg","v","ssv","sssv","ssv"]
+UP3 = ["v","s","s","sssv","sssv","ssv","ssv","s"]
+DOWNS = [["g","g"],["v","g"],["v","s"],["s","s"],["s","s"],["g","s"],["s","s"],["s","s"]]
+ORDER = ["o0","x0","x2","x1","d0","b0","b1","A0","d1","a1","b2","a2","d2","d3","a3","b3","a4","b4","d4","g0","a5","b5","a6","d5","b6","b7","d6","a7","r0","d7","r1","r2"]
+STEPS = ["x0","x2","x1","G0","d0","b0","b1","a0","d1","h0","y0","a1","b2","G1","a2","h1","d2","d3","a3","y1","h2","b3","a4","h3","b4","s0","d4","y2","a5","y3","b5","s1","h4","h5","a6","d5","b6","b7","y4","d6","y5","h6","a7","s2","d7","y6","h7","y7","s3","s4"]
+BUFS = [9,4,3,1,2,1,3,8]
 GATHERS = ((0, 256), (256, 1024))
-SCATTERS = {1: ((0, 256),), 3: ((256, 512),), 5: ((512, 704),), 6: ((704, 864),), 7: ((864, 1024),)}
+SCATTERS = ((0, 256), (256, 512), (512, 704), (704, 864), (864, 1024))
 
 
 def tile_moe_res_glu_silu_kernel(tc, xT, xr, w1, w3, w2, gate, offs, out):
     nc = tc.nc
     with ExitStack() as ctx:
         held = ctx.enter_context(tc.tile_pool(name="held", bufs=1))
-        raw = ctx.enter_context(tc.tile_pool(name="raw", bufs=8))
-        mid = ctx.enter_context(tc.tile_pool(name="mid", bufs=3))
-        cod = ctx.enter_context(tc.tile_pool(name="cod", bufs=3))
+        raw = ctx.enter_context(tc.tile_pool(name="raw", bufs=2))
+        mid = ctx.enter_context(tc.tile_pool(name="mid", bufs=2))
+        cod = ctx.enter_context(tc.tile_pool(name="cod", bufs=2))
         ps = ctx.enter_context(tc.psum_pool(name="ps", bufs=2))
 
         offsets = held.tile([P, S // 16], U16, name="offsets")
@@ -47,42 +49,30 @@ def tile_moe_res_glu_silu_kernel(tc, xT, xr, w1, w3, w2, gate, offs, out):
         res = [held.tile([P, T], F32, name=f"res{b}") for b in range(3)]
         g_codes = [held.tile([P, g1 - g0], U32, name=f"g_codes{g0}", align_bytes=64) for g0, g1 in GATHERS]
         g_scales = [held.tile([P, g1 - g0], U8, name=f"g_scales{g0}", align_bytes=64) for g0, g1 in GATHERS]
+        loaded = {}
 
-        x_raw = {}
-        w1_raw, w3_raw, w2_raw = {}, {}, {}
-
-        def load_x(i):
-            c0, c1 = XT_CHUNKS[i]
-            t = raw.tile([P, 4, H], F32, name="raw_up", bufs=9)
-            x_raw[i] = t
-            nc.sync.dma_start(out=t[:, :, 0 : c1 - c0], in_=xT.rearrange("(p j) t -> p j t", j=4)[:, :, c0:c1])
-
-        def load_up(dst, w, e, parts):
-            t = raw.tile([P, 4, H], F32, name="raw_up", bufs=9)
-            dst[e] = t
-            view = w[e].rearrange("(p j) i -> p j i", j=4)
-            step = H // parts
-            for q in range(parts):
-                nc.sync.dma_start(out=t[:, :, q * step : (q + 1) * step], in_=view[:, :, q * step : (q + 1) * step])
-
-        def load_down(e):
-            t = raw.tile([P, 4, N], F32, name="raw_down", bufs=4)
-            w2_raw[e] = t
-            nc.sync.dma_start(out=t[:], in_=w2[e].rearrange("(p j) n -> p j n", j=4))
-
-        for item in ORDER:
-            k, i = item[0], int(item[1:])
-            if k == "x":
-                load_x(i)
-            elif k == "a" or k == "A":
-                load_up(w1_raw, w1, i, 2 if k == "A" else 1)
-            elif k == "b" or k == "B":
-                load_up(w3_raw, w3, i, 2 if k == "B" else 1)
-            elif k == "d":
-                load_down(i)
-            elif k == "o":
+        def load(item):
+            kind, i = item[0], int(item[1:])
+            if kind == "x":
+                c0, c1 = XT_CHUNKS[i]
+                t = raw.tile([P, 4, H], F32, name="raw_up", bufs=BUFS[0])
+                nc.sync.dma_start(out=t[:, :, 0 : c1 - c0], in_=xT.rearrange("(p j) t -> p j t", j=4)[:, :, c0:c1])
+                loaded[item] = t
+            elif kind in "abAB":
+                w = w1 if kind in "aA" else w3
+                t = raw.tile([P, 4, H], F32, name="raw_up", bufs=BUFS[0])
+                view = w[i].rearrange("(p j) i -> p j i", j=4)
+                step = H if kind in "ab" else H // 2
+                for q in range(0, H, step):
+                    nc.sync.dma_start(out=t[:, :, q : q + step], in_=view[:, :, q : q + step])
+                loaded[("a" if kind in "aA" else "b") + item[1:]] = t
+            elif kind == "d":
+                t = raw.tile([P, 4, N], F32, name="raw_down", bufs=BUFS[1])
+                nc.sync.dma_start(out=t[:], in_=w2[i].rearrange("(p j) n -> p j n", j=4))
+                loaded[item] = t
+            elif kind == "o":
                 nc.sync.dma_start(offsets[:], offs)
-            elif k == "g":
+            elif kind == "g":
                 nc.sync.dma_start(out=gate_sb[:], in_=gate[0:P, :])
             else:
                 nc.sync.dma_start(out=res[i][:], in_=xr[i * P : (i + 1) * P, :])
@@ -106,14 +96,19 @@ def tile_moe_res_glu_silu_kernel(tc, xT, xr, w1, w3, w2, gate, offs, out):
                 r = q
                 while r < len(engines) and engines[r] == engines[q]:
                     r += 1
-                move(engines[q], dst[:, q * step : (count if r == len(engines) else r * step)], src[:, q * step : (count if r == len(engines) else r * step)])
+                stop = count if r == len(engines) else r * step
+                move(engines[q], dst[:, q * step : stop], src[:, q * step : stop])
                 q = r
 
-        for i, (c0, c1) in enumerate(XT_CHUNKS):
+        def natural(t):
+            return t.rearrange("p (c i j) -> p c j i", i=4, j=4)
+
+        def tokens(i):
+            c0, c1 = XT_CHUNKS[i]
             w = c1 - c0
-            x = x_raw[i]
-            xb = mid.tile([P, 4 * H], BF16, name="bf_up", bufs=7, align_bytes=64)
-            spread(X_ENG[i], xb[:, 0 : 4 * w].rearrange("p (c i j) -> p c j i", i=4, j=4), x[:, :, 0:w].rearrange("p j (c i) -> p c j i", i=4), w // 4)
+            x = loaded[f"x{i}"]
+            xb = mid.tile([P, 4 * H], BF16, name="bf_up", bufs=BUFS[2], align_bytes=64)
+            spread(X_ENG[i], natural(xb[:, 0 : 4 * w]), x[:, :, 0:w].rearrange("p j (c i) -> p c j i", i=4), w // 4)
             nc.vector.quantize_mx(out=x_codes[:, c0:c1].bitcast(FP8X4), scales=x_scales[:, c0:c1], in_=xb[:, 0 : 4 * w])
 
         def gather(i):
@@ -123,74 +118,90 @@ def tile_moe_res_glu_silu_kernel(tc, xT, xr, w1, w3, w2, gate, offs, out):
             nc.vector.tensor_copy(out=g_scales[i][:], in_=x_scales[:].indirect(cols))
 
         def slot_operand(e):
-            for i, (g0, g1) in enumerate(GATHERS):
-                if g0 <= e * C < g1:
-                    a = e * C - g0
-                    return g_codes[i][:, a : a + C].bitcast(FP8X4), g_scales[i][:, a : a + C]
+            i = [q for q, (g0, g1) in enumerate(GATHERS) if g0 <= e * C < g1][0]
+            a = e * C - GATHERS[i][0]
+            return g_codes[i][:, a : a + C].bitcast(FP8X4), g_scales[i][:, a : a + C]
 
-        def quantize_up(w_raw, tag, engines):
-            wb = mid.tile([P, 4 * H], BF16, name="bf_up", bufs=7, align_bytes=64)
-            dst = wb[:].rearrange("p (t m j) -> p m j t", t=4, j=4)
-            src = w_raw[:].rearrange("p j (m t) -> p m j t", t=4)
-            spread(engines, dst, src, P)
-            codes = cod.tile([P, H], U32, name=f"codes_{tag}", align_bytes=64)
-            scales = cod.tile([P, H], U8, name=f"scales_{tag}", align_bytes=64)
+        def quantize_up(key, tag, engines):
+            wb = mid.tile([P, 4 * H], BF16, name="bf_up", bufs=BUFS[2], align_bytes=64)
+            spread(engines, wb[:].rearrange("p (t m j) -> p m j t", t=4, j=4), loaded[key][:].rearrange("p j (m t) -> p m j t", t=4), P)
+            codes = cod.tile([P, H], U32, name=f"codes_{tag}", bufs=BUFS[4], align_bytes=64)
+            scales = cod.tile([P, H], U8, name=f"scales_{tag}", bufs=BUFS[4], align_bytes=64)
             nc.vector.quantize_mx(out=codes[:].bitcast(FP8X4), scales=scales[:], in_=wb[:])
             return codes, scales
 
-        def product(bank, codes, scales, x, blocks):
+        def quantize_down(e):
+            codes = cod.tile([P, N], U32, name="codes_down", bufs=BUFS[5], align_bytes=64)
+            scales = cod.tile([P, N], U8, name="scales_down", bufs=BUFS[5], align_bytes=64)
+            src = loaded[f"d{e}"]
+            for part, (c0, c1) in enumerate(((0, 256), (256, 384))):
+                wb = mid.tile([P, 4 * (c1 - c0)], BF16, name="turn", bufs=BUFS[6], align_bytes=64) if part == 0 and e < BUFS[7] else mid.tile([P, 4 * (c1 - c0)], BF16, name=f"bf_down{c0}", bufs=BUFS[3], align_bytes=64)
+                spread(DOWNS[e][part], natural(wb[:]), src[:, :, c0:c1].rearrange("p j (c i) -> p c j i", i=4), (c1 - c0) // 4)
+                nc.vector.quantize_mx(out=codes[:, c0:c1].bitcast(FP8X4), scales=scales[:, c0:c1], in_=wb[:])
+            return codes, scales
+
+        def product(bank, operand, x, blocks):
+            codes, scales = operand
             for t in range(blocks):
                 cols = slice(t * P, (t + 1) * P)
                 nc.tensor.matmul_mx(
                     out=bank[:, t, :], lhsT=codes[:, cols].bitcast(FP8X4), lhsT_scale=scales[:, cols],
                     rhs=x[0], rhs_scale=x[1], start=True, stop=True)
 
-        def down(e, h):
-            w2b = mid.tile([P, 4 * N], BF16, name="bf_down", align_bytes=64)
-            dst = w2b[:].rearrange("p (c i j) -> p c j i", i=4, j=4)
-            src = w2_raw[e][:].rearrange("p j (c i) -> p c j i", i=4)
-            spread(DOWN[e], dst, src, N // 4)
-            codes = cod.tile([P, N], U32, name="codes_down", align_bytes=64)
-            scales = cod.tile([P, N], U8, name="scales_down", align_bytes=64)
-            for c0, c1 in ((0, 256), (256, 384)):
-                nc.vector.quantize_mx(out=codes[:, c0:c1].bitcast(FP8X4), scales=scales[:, c0:c1], in_=w2b[:, 4 * c0 : 4 * c1])
-            y_ps = ps.tile([P, 3, C], F32, name="y_ps", bufs=2)
-            product(y_ps, codes, scales, h, 3)
-            nc.vector.tensor_tensor(
-                out=y_sb[:, :, e * C : (e + 1) * C], in0=y_ps[:],
-                in1=gate_sb[:, e * C : (e + 1) * C].unsqueeze(1).to_broadcast([P, 3, C]), op=MULT)
-            for s0, s1 in SCATTERS.get(e, ()):
-                cols = offsets[:, s0 // 16 : s1 // 16]
-                for b in range(3):
-                    nc.vector.tensor_copy(out=windows[b][:].indirect(cols), in_=y_sb[:, b, s0:s1])
-                    if e == E - 1:
-                        nc.vector.tensor_tensor(out=res[b][:], in0=windows[b][:], in1=res[b][:], op=ADD)
-                        nc.sync.dma_start(out=out[b * P : (b + 1) * P, :], in_=res[b][:])
+        up1, up3, dn, hid, banks = {}, {}, {}, {}, {}
 
-        prev = None
-        for e in range(E):
-            c1, s1 = quantize_up(w1_raw[e], "w1", UP1[e])
-            if e == 0:
-                gather(0)
-            c3, s3 = quantize_up(w3_raw[e], "w3", UP3[e])
+        def hidden(e):
             x = slot_operand(e)
             a_ps = ps.tile([P, 4, C], F32, name="a_ps", bufs=3)
             b_ps = ps.tile([P, 4, C], F32, name="b_ps", bufs=3)
-            product(a_ps, c1, s1, x, 4)
-            product(b_ps, c3, s3, x, 4)
+            product(a_ps, up1[e], x, 4)
+            product(b_ps, up3[e], x, 4)
             sil = mid.tile([P, 4, C], F32, name="sil")
             nc.scalar.activation(out=sil[:], in_=a_ps[:], func=SILU)
-            hb = mid.tile([P, 4 * C], BF16, name="hb", align_bytes=64)
+            hb = mid.tile([P, 4 * C], BF16, name="turn", bufs=BUFS[6], align_bytes=64)
             nc.vector.tensor_tensor(
-                out=hb[:].rearrange("p (c i j) -> p c j i", i=4, j=4),
-                in0=b_ps[:].rearrange("p j (c i) -> p c j i", i=4),
+                out=natural(hb[:]), in0=b_ps[:].rearrange("p j (c i) -> p c j i", i=4),
                 in1=sil[:].rearrange("p j (c i) -> p c j i", i=4), op=MULT)
-            if e == 0:
-                gather(1)
             hc = cod.tile([P, C], U32, name="hc", align_bytes=64)
             hs = cod.tile([P, C], U8, name="hs", align_bytes=64)
             nc.vector.quantize_mx(out=hc[:].bitcast(FP8X4), scales=hs[:], in_=hb[:])
-            if e > 0:
-                down(e - 1, prev)
-            prev = (hc[:].bitcast(FP8X4), hs[:])
-        down(E - 1, prev)
+            hid[e] = (hc[:].bitcast(FP8X4), hs[:])
+
+        def result(e):
+            y_ps = ps.tile([P, 3, C], F32, name="y_ps", bufs=2)
+            product(y_ps, dn[e], hid[e], 3)
+            nc.scalar.copy(out=y_sb[:, :, e * C : (e + 1) * C], in_=y_ps[:])
+
+        scattered = []
+
+        def scatter(i):
+            s0, s1 = SCATTERS[i]
+            scattered.append(i)
+            cols = offsets[:, s0 // 16 : s1 // 16]
+            for b in range(3):
+                nc.vector.tensor_tensor(windows[b][:].indirect(cols), y_sb[:, b, s0:s1], gate_sb[:, s0:s1], MULT)
+                if len(scattered) == len(SCATTERS):
+                    for q0, q1 in ((0, T),) if b < 2 else ((0, 896), (896, T)):
+                        (nc.vector).tensor_tensor(out=res[b][:, q0:q1], in0=windows[b][:, q0:q1], in1=res[b][:, q0:q1], op=ADD)
+                        nc.sync.dma_start(out=out[b * P : (b + 1) * P, q0:q1], in_=res[b][:, q0:q1])
+
+        for item in ORDER:
+            load(item)
+        for item in STEPS:
+            kind, i = item[0], int(item[1:])
+            if kind == "x":
+                tokens(i)
+            elif kind == "a":
+                up1[i] = quantize_up(item, "w1", UP1[i])
+            elif kind == "b":
+                up3[i] = quantize_up(item, "w3", UP3[i])
+            elif kind == "d":
+                dn[i] = quantize_down(i)
+            elif kind == "G":
+                gather(i)
+            elif kind == "h":
+                hidden(i)
+            elif kind == "y":
+                result(i)
+            elif kind == "s":
+                scatter(i)

@@ -20,13 +20,12 @@ FLOPS = 2 * S * (2 * K * H + H * N)
 BYTES = 4 * (K * T + N * T + E * K * H * 2 + E * H * N + P * S + N * T) + 2 * P * S // 16
 
 XT_CHUNKS = ((0, 256), (256, 768), (768, 1280))
-X_ENG = ["s","ssv","sssv"]
-UP1 = ["v","sv","s","ssg","v","ssv","sssv","ssv"]
-UP3 = ["v","s","s","sssv","sssv","ssv","ssv","s"]
-DOWNS = [["g","g"],["v","g"],["v","s"],["s","s"],["s","s"],["g","s"],["s","s"],["s","s"]]
-ORDER = ["o0","x0","x2","x1","d0","b0","b1","A0","d1","a1","b2","a2","d2","d3","a3","b3","a4","b4","d4","g0","a5","b5","a6","d5","b6","b7","d6","a7","r0","d7","r1","r2"]
-STEPS = ["x0","x2","x1","G0","d0","b0","b1","a0","d1","h0","y0","a1","b2","G1","a2","h1","d2","d3","a3","y1","h2","b3","a4","h3","b4","s0","d4","y2","a5","y3","b5","s1","h4","h5","a6","d5","b6","b7","y4","d6","y5","h6","a7","s2","d7","y6","h7","y7","s3","s4"]
-BUFS = [9,4,3,1,2,1,3,8]
+X_ENG = ["v","v","v"]
+UP1 = ["s","s","s","s","s","s","s","s"]
+UP3 = ["s","s","s","s","s","s","s","s"]
+DOWN = [[0,0],[0,256],[0,256],[0,256],[0,256],[0,256],[0,256],[0,0]]
+SEQ = ["x0","a0","x1","b0","x2","o0","A0","G0","B0","d0","G1","a1","m0","D0","b1","g0","t0","A1","u0","B1","y0","d1","a2","m1","D1","b2","t1","A2","u1","B2","y1","d2","a3","m2","D2","b3","t2","A3","u2","B3","s0","y2","d3","a4","m3","D3","b4","t3","A4","u3","B4","y3","d4","a5","m4","D4","b5","t4","A5","u4","B5","s1","y4","d5","a6","m5","D5","b6","t5","A6","u5","B6","y5","d6","a7","m6","D6","b7","t6","A7","u6","B7","s2","y6","d7","m7","D7","t7","u7","s3","y7","s4","r0","r1","r2"]
+BUFS = [9,3,6,3,3,3,1,0,3,3,3,3,3,2]
 GATHERS = ((0, 256), (256, 1024))
 SCATTERS = ((0, 256), (256, 512), (512, 704), (704, 864), (864, 1024))
 
@@ -50,6 +49,9 @@ def tile_moe_res_glu_silu_kernel(tc, xT, xr, w1, w3, w2, gate, offs, out):
         g_codes = [held.tile([P, g1 - g0], U32, name=f"g_codes{g0}", align_bytes=64) for g0, g1 in GATHERS]
         g_scales = [held.tile([P, g1 - g0], U8, name=f"g_scales{g0}", align_bytes=64) for g0, g1 in GATHERS]
         loaded = {}
+        one = held.tile([P, 1], F32, name="one")
+        nc.vector.memset(one[:], 1.0)
+        zeros = [held.tile([P, 1], F32, name=f"zero{e}") for e in range(E)]
 
         def load(item):
             kind, i = item[0], int(item[1:])
@@ -81,15 +83,16 @@ def tile_moe_res_glu_silu_kernel(tc, xT, xr, w1, w3, w2, gate, offs, out):
         for b in range(3):
             nc.vector.memset(windows[b][:], 0.0)
 
-        def move(engine, dst, src):
+        def move(engine, dst, src, natural_order):
             if engine == "s":
                 nc.scalar.activation(out=dst, in_=src, func=COPY)
             elif engine == "g":
-                nc.gpsimd.tensor_scalar(out=dst, in0=src, scalar1=1.0, scalar2=0.0, op0=MULT, op1=ADD)
+                order = "p c j i -> p c i j" if natural_order else "p m j t -> p t m j"
+                nc.gpsimd.tensor_scalar(out=dst.rearrange(order), in0=src.rearrange(order), scalar1=1.0, scalar2=0.0, op0=MULT, op1=ADD)
             else:
                 nc.vector.tensor_copy(out=dst, in_=src)
 
-        def spread(engines, dst, src, count):
+        def spread(engines, dst, src, count, natural_order=True):
             step = count // len(engines)
             q = 0
             while q < len(engines):
@@ -97,7 +100,7 @@ def tile_moe_res_glu_silu_kernel(tc, xT, xr, w1, w3, w2, gate, offs, out):
                 while r < len(engines) and engines[r] == engines[q]:
                     r += 1
                 stop = count if r == len(engines) else r * step
-                move(engines[q], dst[:, q * step : stop], src[:, q * step : stop])
+                move(engines[q], dst[:, q * step : stop], src[:, q * step : stop], natural_order)
                 q = r
 
         def natural(t):
@@ -124,20 +127,37 @@ def tile_moe_res_glu_silu_kernel(tc, xT, xr, w1, w3, w2, gate, offs, out):
 
         def quantize_up(key, tag, engines):
             wb = mid.tile([P, 4 * H], BF16, name="bf_up", bufs=BUFS[2], align_bytes=64)
-            spread(engines, wb[:].rearrange("p (t m j) -> p m j t", t=4, j=4), loaded[key][:].rearrange("p j (m t) -> p m j t", t=4), P)
+            spread(engines, wb[:].rearrange("p (t m j) -> p m j t", t=4, j=4), loaded[key][:].rearrange("p j (m t) -> p m j t", t=4), P, False)
+            return wb
+
+        def codes_up(wb, tag):
             codes = cod.tile([P, H], U32, name=f"codes_{tag}", bufs=BUFS[4], align_bytes=64)
             scales = cod.tile([P, H], U8, name=f"scales_{tag}", bufs=BUFS[4], align_bytes=64)
             nc.vector.quantize_mx(out=codes[:].bitcast(FP8X4), scales=scales[:], in_=wb[:])
             return codes, scales
 
-        def quantize_down(e):
+        def lay_down(e):
+            wb = mid.tile([P, 4 * N], BF16, name="bf_down", bufs=BUFS[3], align_bytes=64)
+            src = loaded[f"d{e}"]
+            cut = DOWN[e][0] + DOWN[e][1]
+            for q in range(0, DOWN[e][0], 128):
+                nc.gpsimd.tensor_scalar(
+                    out=wb[:, 4 * q : 4 * (q + 128)].rearrange("p (c j) -> p c j", j=4), in0=src[:, :, q : q + 128].rearrange("p j c -> p c j"),
+                    scalar1=one[:], scalar2=zeros[e][:], op0=MULT, op1=ADD)
+            if DOWN[e][1]:
+                q = DOWN[e][0]
+                nc.vector.tensor_scalar(
+                    out=natural(wb[:, 4 * q : 4 * cut]), in0=src[:, :, q:cut].rearrange("p j (c i) -> p c j i", i=4),
+                    scalar1=one[:], scalar2=zeros[e][:], op0=MULT, op1=ADD)
+            if cut < N:
+                move("s", natural(wb[:, 4 * cut :]), src[:, :, cut:].rearrange("p j (c i) -> p c j i", i=4), True)
+            return wb
+
+        def codes_down(wb):
             codes = cod.tile([P, N], U32, name="codes_down", bufs=BUFS[5], align_bytes=64)
             scales = cod.tile([P, N], U8, name="scales_down", bufs=BUFS[5], align_bytes=64)
-            src = loaded[f"d{e}"]
-            for part, (c0, c1) in enumerate(((0, 256), (256, 384))):
-                wb = mid.tile([P, 4 * (c1 - c0)], BF16, name="turn", bufs=BUFS[6], align_bytes=64) if part == 0 and e < BUFS[7] else mid.tile([P, 4 * (c1 - c0)], BF16, name=f"bf_down{c0}", bufs=BUFS[3], align_bytes=64)
-                spread(DOWNS[e][part], natural(wb[:]), src[:, :, c0:c1].rearrange("p j (c i) -> p c j i", i=4), (c1 - c0) // 4)
-                nc.vector.quantize_mx(out=codes[:, c0:c1].bitcast(FP8X4), scales=scales[:, c0:c1], in_=wb[:])
+            for c0, c1 in ((0, 256), (256, 384)):
+                nc.vector.quantize_mx(out=codes[:, c0:c1].bitcast(FP8X4), scales=scales[:, c0:c1], in_=wb[:, 4 * c0 : 4 * c1])
             return codes, scales
 
         def product(bank, operand, x, blocks):
@@ -150,27 +170,35 @@ def tile_moe_res_glu_silu_kernel(tc, xT, xr, w1, w3, w2, gate, offs, out):
 
         up1, up3, dn, hid, banks = {}, {}, {}, {}, {}
 
-        def hidden(e):
+        def first_products(e):
             x = slot_operand(e)
-            a_ps = ps.tile([P, 4, C], F32, name="a_ps", bufs=3)
-            b_ps = ps.tile([P, 4, C], F32, name="b_ps", bufs=3)
+            a_ps = ps.tile([P, 4, C], F32, name="a_ps", bufs=BUFS[11])
+            b_ps = ps.tile([P, 4, C], F32, name="b_ps", bufs=BUFS[12])
             product(a_ps, up1[e], x, 4)
             product(b_ps, up3[e], x, 4)
-            sil = mid.tile([P, 4, C], F32, name="sil")
+            sil = mid.tile([P, 4, C], F32, name="sil", bufs=BUFS[8])
             nc.scalar.activation(out=sil[:], in_=a_ps[:], func=SILU)
-            hb = mid.tile([P, 4 * C], BF16, name="turn", bufs=BUFS[6], align_bytes=64)
+            return b_ps, sil
+
+        def gated(b_ps, sil):
+            hb = mid.tile([P, 4 * C], BF16, name="hb", bufs=BUFS[9], align_bytes=64)
             nc.vector.tensor_tensor(
                 out=natural(hb[:]), in0=b_ps[:].rearrange("p j (c i) -> p c j i", i=4),
                 in1=sil[:].rearrange("p j (c i) -> p c j i", i=4), op=MULT)
-            hc = cod.tile([P, C], U32, name="hc", align_bytes=64)
-            hs = cod.tile([P, C], U8, name="hs", align_bytes=64)
+            return hb
+
+        def codes_hidden(hb):
+            hc = cod.tile([P, C], U32, name="hc", bufs=BUFS[10], align_bytes=64)
+            hs = cod.tile([P, C], U8, name="hs", bufs=BUFS[10], align_bytes=64)
             nc.vector.quantize_mx(out=hc[:].bitcast(FP8X4), scales=hs[:], in_=hb[:])
-            hid[e] = (hc[:].bitcast(FP8X4), hs[:])
+            return hc[:].bitcast(FP8X4), hs[:]
 
         def result(e):
-            y_ps = ps.tile([P, 3, C], F32, name="y_ps", bufs=2)
+            y_ps = ps.tile([P, 3, C], F32, name="y_ps", bufs=BUFS[13])
             product(y_ps, dn[e], hid[e], 3)
-            nc.scalar.copy(out=y_sb[:, :, e * C : (e + 1) * C], in_=y_ps[:])
+            nc.vector.tensor_tensor(
+                out=y_sb[:, :, e * C : (e + 1) * C], in0=y_ps[:],
+                in1=gate_sb[:, e * C : (e + 1) * C].unsqueeze(1).to_broadcast([P, 3, C]), op=MULT)
 
         scattered = []
 
@@ -179,28 +207,42 @@ def tile_moe_res_glu_silu_kernel(tc, xT, xr, w1, w3, w2, gate, offs, out):
             scattered.append(i)
             cols = offsets[:, s0 // 16 : s1 // 16]
             for b in range(3):
-                nc.vector.tensor_tensor(windows[b][:].indirect(cols), y_sb[:, b, s0:s1], gate_sb[:, s0:s1], MULT)
+                nc.vector.tensor_copy(out=windows[b][:].indirect(cols), in_=y_sb[:, b, s0:s1])
                 if len(scattered) == len(SCATTERS):
                     for q0, q1 in ((0, T),) if b < 2 else ((0, 896), (896, T)):
                         (nc.vector).tensor_tensor(out=res[b][:, q0:q1], in0=windows[b][:, q0:q1], in1=res[b][:, q0:q1], op=ADD)
                         nc.sync.dma_start(out=out[b * P : (b + 1) * P, q0:q1], in_=res[b][:, q0:q1])
 
-        for item in ORDER:
-            load(item)
-        for item in STEPS:
+        for item in SEQ:
+            if item[0] in "xabdogr":
+                load("A0" if item == "a0" else item)
+        la, lb, ld, pr, hb = {}, {}, {}, {}, {}
+        for item in SEQ:
             kind, i = item[0], int(item[1:])
             if kind == "x":
                 tokens(i)
             elif kind == "a":
-                up1[i] = quantize_up(item, "w1", UP1[i])
+                la[i] = quantize_up(item, "w1", UP1[i])
             elif kind == "b":
-                up3[i] = quantize_up(item, "w3", UP3[i])
+                lb[i] = quantize_up(item, "w3", UP3[i])
+                if DOWN[i][0] or DOWN[i][1]:
+                    nc.scalar.mul(zeros[i][:], lb[i][:, 0:1], 0.0)
             elif kind == "d":
-                dn[i] = quantize_down(i)
+                ld[i] = lay_down(i)
+            elif kind == "A":
+                up1[i] = codes_up(la[i], "w1")
+            elif kind == "B":
+                up3[i] = codes_up(lb[i], "w3")
+            elif kind == "D":
+                dn[i] = codes_down(ld[i])
             elif kind == "G":
                 gather(i)
-            elif kind == "h":
-                hidden(i)
+            elif kind == "m":
+                pr[i] = first_products(i)
+            elif kind == "t":
+                hb[i] = gated(pr[i][0], pr[i][1])
+            elif kind == "u":
+                hid[i] = codes_hidden(hb[i])
             elif kind == "y":
                 result(i)
             elif kind == "s":

@@ -23,9 +23,10 @@ XT_CHUNKS = ((0, 256), (256, 768), (768, 1280))
 X_ENG = ["v","v","v"]
 UP1 = ["s","s","s","s","s","s","s","s"]
 UP3 = ["s","s","s","s","s","s","s","s"]
-DOWN = [[0,0],[0,256],[0,256],[0,256],[0,256],[0,256],[0,256],[0,0]]
-SEQ = ["x0","a0","x1","b0","x2","o0","A0","G0","B0","d0","G1","a1","m0","D0","b1","g0","t0","A1","u0","B1","y0","d1","a2","m1","D1","b2","t1","A2","u1","B2","y1","d2","a3","m2","D2","b3","t2","A3","u2","B3","s0","y2","d3","a4","m3","D3","b4","t3","A4","u3","B4","y3","d4","a5","m4","D4","b5","t4","A5","u4","B5","s1","y4","d5","a6","m5","D5","b6","t5","A6","u5","B6","y5","d6","a7","m6","D6","b7","t6","A7","u6","B7","s2","y6","d7","m7","D7","t7","u7","s3","y7","s4","r0","r1","r2"]
+DOWN = [[0,0],[0,256],[0,256],[0,256],[0,256],[0,256],[0,256],[0,256]]
+SEQ = ["a0","x0","b0","x1","x2","o0","A0","G0","B0","d0","G1","p0","D0","a1","b1","g0","m0","t0","A1","u0","B1","d1","a2","p1","D1","b2","m1","y0","t1","A2","u1","B2","d2","a3","p2","D2","b3","m2","y1","t2","A3","u2","B3","s0","d3","a4","p3","D3","b4","m3","y2","t3","A4","u3","B4","d4","a5","p4","D4","b5","m4","y3","t4","A5","u4","B5","s1","d5","a6","p5","D5","b6","m5","y4","t5","A6","u5","B6","d6","a7","p6","D6","b7","m6","y5","t6","A7","u6","B7","s2","d7","p7","D7","m7","y6","t7","u7","s3","y7","s4","r0","r1","r2"]
 BUFS = [9,3,6,3,3,3,1,0,3,3,3,3,3,2]
+MARKS = [1,2,3,4,5,6,7]
 GATHERS = ((0, 256), (256, 1024))
 SCATTERS = ((0, 256), (256, 512), (512, 704), (704, 864), (864, 1024))
 
@@ -176,9 +177,12 @@ def tile_moe_res_glu_silu_kernel(tc, xT, xr, w1, w3, w2, gate, offs, out):
             b_ps = ps.tile([P, 4, C], F32, name="b_ps", bufs=BUFS[12])
             product(a_ps, up1[e], x, 4)
             product(b_ps, up3[e], x, 4)
+            return a_ps, b_ps
+
+        def silu_of(a_ps, mark):
             sil = mid.tile([P, 4, C], F32, name="sil", bufs=BUFS[8])
-            nc.scalar.activation(out=sil[:], in_=a_ps[:], func=SILU)
-            return b_ps, sil
+            nc.scalar.activation(out=sil[:], in_=a_ps[:], func=SILU, bias=zeros[mark][:] if mark in MARKS else 0.0)
+            return sil
 
         def gated(b_ps, sil):
             hb = mid.tile([P, 4 * C], BF16, name="hb", bufs=BUFS[9], align_bytes=64)
@@ -196,9 +200,9 @@ def tile_moe_res_glu_silu_kernel(tc, xT, xr, w1, w3, w2, gate, offs, out):
         def result(e):
             y_ps = ps.tile([P, 3, C], F32, name="y_ps", bufs=BUFS[13])
             product(y_ps, dn[e], hid[e], 3)
-            nc.vector.tensor_tensor(
-                out=y_sb[:, :, e * C : (e + 1) * C], in0=y_ps[:],
-                in1=gate_sb[:, e * C : (e + 1) * C].unsqueeze(1).to_broadcast([P, 3, C]), op=MULT)
+            nc.scalar.activation(
+                out=y_sb[:, :, e * C : (e + 1) * C], in_=y_ps[:], func=mybir.ActivationFunctionType.Identity,
+                bias=zeros[e + 2][:] if e + 2 in MARKS else 0.0)
 
         scattered = []
 
@@ -207,7 +211,7 @@ def tile_moe_res_glu_silu_kernel(tc, xT, xr, w1, w3, w2, gate, offs, out):
             scattered.append(i)
             cols = offsets[:, s0 // 16 : s1 // 16]
             for b in range(3):
-                nc.vector.tensor_copy(out=windows[b][:].indirect(cols), in_=y_sb[:, b, s0:s1])
+                nc.vector.tensor_tensor(windows[b][:].indirect(cols), y_sb[:, b, s0:s1], gate_sb[:, s0:s1], MULT)
                 if len(scattered) == len(SCATTERS):
                     for q0, q1 in ((0, T),) if b < 2 else ((0, 896), (896, T)):
                         (nc.vector).tensor_tensor(out=res[b][:, q0:q1], in0=windows[b][:, q0:q1], in1=res[b][:, q0:q1], op=ADD)
@@ -216,7 +220,7 @@ def tile_moe_res_glu_silu_kernel(tc, xT, xr, w1, w3, w2, gate, offs, out):
         for item in SEQ:
             if item[0] in "xabdogr":
                 load("A0" if item == "a0" else item)
-        la, lb, ld, pr, hb = {}, {}, {}, {}, {}
+        la, lb, ld, pr, hb, si = {}, {}, {}, {}, {}, {}
         for item in SEQ:
             kind, i = item[0], int(item[1:])
             if kind == "x":
@@ -225,8 +229,8 @@ def tile_moe_res_glu_silu_kernel(tc, xT, xr, w1, w3, w2, gate, offs, out):
                 la[i] = quantize_up(item, "w1", UP1[i])
             elif kind == "b":
                 lb[i] = quantize_up(item, "w3", UP3[i])
-                if DOWN[i][0] or DOWN[i][1]:
-                    nc.scalar.mul(zeros[i][:], lb[i][:, 0:1], 0.0)
+                if i in MARKS:
+                    nc.gpsimd.tensor_scalar(out=zeros[i][:], in0=lb[i][:, 0:1], scalar1=0.0, scalar2=0.0, op0=MULT, op1=ADD)
             elif kind == "d":
                 ld[i] = lay_down(i)
             elif kind == "A":
@@ -237,10 +241,12 @@ def tile_moe_res_glu_silu_kernel(tc, xT, xr, w1, w3, w2, gate, offs, out):
                 dn[i] = codes_down(ld[i])
             elif kind == "G":
                 gather(i)
-            elif kind == "m":
+            elif kind == "p":
                 pr[i] = first_products(i)
+            elif kind == "m":
+                si[i] = silu_of(pr[i][0], i + 1)
             elif kind == "t":
-                hb[i] = gated(pr[i][0], pr[i][1])
+                hb[i] = gated(pr[i][1], si[i])
             elif kind == "u":
                 hid[i] = codes_hidden(hb[i])
             elif kind == "y":

from contextlib import ExitStack

import concourse.mybir as mybir

K, T, E, C, H, N = 512, 1280, 8, 128, 512, 384
S = E * C
P = 128
F32 = mybir.dt.float32
BF16 = mybir.dt.bfloat16
U32 = mybir.dt.uint32
U8 = mybir.dt.uint8
U16 = mybir.dt.uint16
FP8X4 = mybir.dt.float8_e4m3fn_x4
COPY = mybir.ActivationFunctionType.Copy
SILU = mybir.ActivationFunctionType.Silu
MULT = mybir.AluOpType.mult
ADD = mybir.AluOpType.add

FLOPS = 2 * S * (2 * K * H + H * N)
BYTES = 4 * (K * T + N * T + E * K * H * 2 + E * H * N + P * S + N * T) + 2 * P * S // 16

XT_CHUNKS = ((0, 256), (256, 768), (768, 1280))
X_ENG = ["v","v","v"]
UP1 = ["s","s","s","s","s","s","s","s"]
UP3 = ["s","s","s","s","s","s","s","s"]
DOWN = [[0,0],[0,256],[0,256],[0,256],[0,256],[0,256],[0,256],[0,256]]
SEQ = ["a0","x0","b0","x1","x2","o0","A0","G0","B0","d0","G1","p0","D0","a1","b1","g0","m0","t0","A1","u0","B1","d1","a2","p1","D1","b2","m1","y0","t1","A2","u1","B2","d2","a3","p2","D2","b3","m2","y1","t2","A3","u2","B3","s0","d3","a4","p3","D3","b4","m3","y2","t3","A4","u3","B4","d4","a5","p4","D4","b5","m4","y3","t4","A5","u4","B5","s1","d5","a6","p5","D5","b6","m5","y4","t5","A6","u5","B6","d6","a7","p6","D6","b7","m6","y5","t6","A7","u6","B7","s2","d7","p7","D7","m7","y6","t7","u7","s3","y7","s4","r0","r1","r2"]
BUFS = [9,3,6,3,3,3,1,0,3,3,3,3,3,2]
MARKS = [1,2,3,4,5,6,7]
GATHERS = ((0, 256), (256, 1024))
SCATTERS = ((0, 256), (256, 512), (512, 704), (704, 864), (864, 1024))


def tile_moe_res_glu_silu_kernel(tc, xT, xr, w1, w3, w2, gate, offs, out):
    nc = tc.nc
    with ExitStack() as ctx:
        held = ctx.enter_context(tc.tile_pool(name="held", bufs=1))
        raw = ctx.enter_context(tc.tile_pool(name="raw", bufs=2))
        mid = ctx.enter_context(tc.tile_pool(name="mid", bufs=2))
        cod = ctx.enter_context(tc.tile_pool(name="cod", bufs=2))
        ps = ctx.enter_context(tc.psum_pool(name="ps", bufs=2))

        offsets = held.tile([P, S // 16], U16, name="offsets")
        gate_sb = held.tile([P, S], F32, name="gate_sb")
        x_codes = held.tile([P, T], U32, name="x_codes", align_bytes=64)
        x_scales = held.tile([P, T], U8, name="x_scales", align_bytes=64)
        y_sb = held.tile([P, 3, S], F32, name="y_sb")
        windows = [held.tile([P, T], F32, name=f"window{b}") for b in range(3)]
        res = [held.tile([P, T], F32, name=f"res{b}") for b in range(3)]
        g_codes = [held.tile([P, g1 - g0], U32, name=f"g_codes{g0}", align_bytes=64) for g0, g1 in GATHERS]
        g_scales = [held.tile([P, g1 - g0], U8, name=f"g_scales{g0}", align_bytes=64) for g0, g1 in GATHERS]
        loaded = {}
        one = held.tile([P, 1], F32, name="one")
        nc.vector.memset(one[:], 1.0)
        zeros = [held.tile([P, 1], F32, name=f"zero{e}") for e in range(E)]

        def load(item):
            kind, i = item[0], int(item[1:])
            if kind == "x":
                c0, c1 = XT_CHUNKS[i]
                t = raw.tile([P, 4, H], F32, name="raw_up", bufs=BUFS[0])
                nc.sync.dma_start(out=t[:, :, 0 : c1 - c0], in_=xT.rearrange("(p j) t -> p j t", j=4)[:, :, c0:c1])
                loaded[item] = t
            elif kind in "abAB":
                w = w1 if kind in "aA" else w3
                t = raw.tile([P, 4, H], F32, name="raw_up", bufs=BUFS[0])
                view = w[i].rearrange("(p j) i -> p j i", j=4)
                step = H if kind in "ab" else H // 2
                for q in range(0, H, step):
                    nc.sync.dma_start(out=t[:, :, q : q + step], in_=view[:, :, q : q + step])
                loaded[("a" if kind in "aA" else "b") + item[1:]] = t
            elif kind == "d":
                t = raw.tile([P, 4, N], F32, name="raw_down", bufs=BUFS[1])
                nc.sync.dma_start(out=t[:], in_=w2[i].rearrange("(p j) n -> p j n", j=4))
                loaded[item] = t
            elif kind == "o":
                nc.sync.dma_start(offsets[:], offs)
            elif kind == "g":
                nc.sync.dma_start(out=gate_sb[:], in_=gate[0:P, :])
            else:
                nc.sync.dma_start(out=res[i][:], in_=xr[i * P : (i + 1) * P, :])

        nc.gpsimd.memset(x_scales[:], 0)
        for b in range(3):
            nc.vector.memset(windows[b][:], 0.0)

        def move(engine, dst, src, natural_order):
            if engine == "s":
                nc.scalar.activation(out=dst, in_=src, func=COPY)
            elif engine == "g":
                order = "p c j i -> p c i j" if natural_order else "p m j t -> p t m j"
                nc.gpsimd.tensor_scalar(out=dst.rearrange(order), in0=src.rearrange(order), scalar1=1.0, scalar2=0.0, op0=MULT, op1=ADD)
            else:
                nc.vector.tensor_copy(out=dst, in_=src)

        def spread(engines, dst, src, count, natural_order=True):
            step = count // len(engines)
            q = 0
            while q < len(engines):
                r = q
                while r < len(engines) and engines[r] == engines[q]:
                    r += 1
                stop = count if r == len(engines) else r * step
                move(engines[q], dst[:, q * step : stop], src[:, q * step : stop], natural_order)
                q = r

        def natural(t):
            return t.rearrange("p (c i j) -> p c j i", i=4, j=4)

        def tokens(i):
            c0, c1 = XT_CHUNKS[i]
            w = c1 - c0
            x = loaded[f"x{i}"]
            xb = mid.tile([P, 4 * H], BF16, name="bf_up", bufs=BUFS[2], align_bytes=64)
            spread(X_ENG[i], natural(xb[:, 0 : 4 * w]), x[:, :, 0:w].rearrange("p j (c i) -> p c j i", i=4), w // 4)
            nc.vector.quantize_mx(out=x_codes[:, c0:c1].bitcast(FP8X4), scales=x_scales[:, c0:c1], in_=xb[:, 0 : 4 * w])

        def gather(i):
            g0, g1 = GATHERS[i]
            cols = offsets[:, g0 // 16 : g1 // 16]
            nc.vector.tensor_copy(out=g_codes[i][:], in_=x_codes[:].indirect(cols))
            nc.vector.tensor_copy(out=g_scales[i][:], in_=x_scales[:].indirect(cols))

        def slot_operand(e):
            i = [q for q, (g0, g1) in enumerate(GATHERS) if g0 <= e * C < g1][0]
            a = e * C - GATHERS[i][0]
            return g_codes[i][:, a : a + C].bitcast(FP8X4), g_scales[i][:, a : a + C]

        def quantize_up(key, tag, engines):
            wb = mid.tile([P, 4 * H], BF16, name="bf_up", bufs=BUFS[2], align_bytes=64)
            spread(engines, wb[:].rearrange("p (t m j) -> p m j t", t=4, j=4), loaded[key][:].rearrange("p j (m t) -> p m j t", t=4), P, False)
            return wb

        def codes_up(wb, tag):
            codes = cod.tile([P, H], U32, name=f"codes_{tag}", bufs=BUFS[4], align_bytes=64)
            scales = cod.tile([P, H], U8, name=f"scales_{tag}", bufs=BUFS[4], align_bytes=64)
            nc.vector.quantize_mx(out=codes[:].bitcast(FP8X4), scales=scales[:], in_=wb[:])
            return codes, scales

        def lay_down(e):
            wb = mid.tile([P, 4 * N], BF16, name="bf_down", bufs=BUFS[3], align_bytes=64)
            src = loaded[f"d{e}"]
            cut = DOWN[e][0] + DOWN[e][1]
            for q in range(0, DOWN[e][0], 128):
                nc.gpsimd.tensor_scalar(
                    out=wb[:, 4 * q : 4 * (q + 128)].rearrange("p (c j) -> p c j", j=4), in0=src[:, :, q : q + 128].rearrange("p j c -> p c j"),
                    scalar1=one[:], scalar2=zeros[e][:], op0=MULT, op1=ADD)
            if DOWN[e][1]:
                q = DOWN[e][0]
                nc.vector.tensor_scalar(
                    out=natural(wb[:, 4 * q : 4 * cut]), in0=src[:, :, q:cut].rearrange("p j (c i) -> p c j i", i=4),
                    scalar1=one[:], scalar2=zeros[e][:], op0=MULT, op1=ADD)
            if cut < N:
                move("s", natural(wb[:, 4 * cut :]), src[:, :, cut:].rearrange("p j (c i) -> p c j i", i=4), True)
            return wb

        def codes_down(wb):
            codes = cod.tile([P, N], U32, name="codes_down", bufs=BUFS[5], align_bytes=64)
            scales = cod.tile([P, N], U8, name="scales_down", bufs=BUFS[5], align_bytes=64)
            for c0, c1 in ((0, 256), (256, 384)):
                nc.vector.quantize_mx(out=codes[:, c0:c1].bitcast(FP8X4), scales=scales[:, c0:c1], in_=wb[:, 4 * c0 : 4 * c1])
            return codes, scales

        def product(bank, operand, x, blocks):
            codes, scales = operand
            for t in range(blocks):
                cols = slice(t * P, (t + 1) * P)
                nc.tensor.matmul_mx(
                    out=bank[:, t, :], lhsT=codes[:, cols].bitcast(FP8X4), lhsT_scale=scales[:, cols],
                    rhs=x[0], rhs_scale=x[1], start=True, stop=True)

        up1, up3, dn, hid, banks = {}, {}, {}, {}, {}

        def first_products(e):
            x = slot_operand(e)
            a_ps = ps.tile([P, 4, C], F32, name="a_ps", bufs=BUFS[11])
            b_ps = ps.tile([P, 4, C], F32, name="b_ps", bufs=BUFS[12])
            product(a_ps, up1[e], x, 4)
            product(b_ps, up3[e], x, 4)
            return a_ps, b_ps

        def silu_of(a_ps, mark):
            sil = mid.tile([P, 4, C], F32, name="sil", bufs=BUFS[8])
            nc.scalar.activation(out=sil[:], in_=a_ps[:], func=SILU, bias=zeros[mark][:] if mark in MARKS else 0.0)
            return sil

        def gated(b_ps, sil):
            hb = mid.tile([P, 4 * C], BF16, name="hb", bufs=BUFS[9], align_bytes=64)
            nc.vector.tensor_tensor(
                out=natural(hb[:]), in0=b_ps[:].rearrange("p j (c i) -> p c j i", i=4),
                in1=sil[:].rearrange("p j (c i) -> p c j i", i=4), op=MULT)
            return hb

        def codes_hidden(hb):
            hc = cod.tile([P, C], U32, name="hc", bufs=BUFS[10], align_bytes=64)
            hs = cod.tile([P, C], U8, name="hs", bufs=BUFS[10], align_bytes=64)
            nc.vector.quantize_mx(out=hc[:].bitcast(FP8X4), scales=hs[:], in_=hb[:])
            return hc[:].bitcast(FP8X4), hs[:]

        def result(e):
            y_ps = ps.tile([P, 3, C], F32, name="y_ps", bufs=BUFS[13])
            product(y_ps, dn[e], hid[e], 3)
            nc.scalar.activation(
                out=y_sb[:, :, e * C : (e + 1) * C], in_=y_ps[:], func=mybir.ActivationFunctionType.Identity,
                bias=zeros[e + 2][:] if e + 2 in MARKS else 0.0)

        scattered = []

        def scatter(i):
            s0, s1 = SCATTERS[i]
            scattered.append(i)
            cols = offsets[:, s0 // 16 : s1 // 16]
            for b in range(3):
                nc.vector.tensor_tensor(windows[b][:].indirect(cols), y_sb[:, b, s0:s1], gate_sb[:, s0:s1], MULT)
                if len(scattered) == len(SCATTERS):
                    for q0, q1 in ((0, T),) if b < 2 else ((0, 896), (896, T)):
                        (nc.vector).tensor_tensor(out=res[b][:, q0:q1], in0=windows[b][:, q0:q1], in1=res[b][:, q0:q1], op=ADD)
                        nc.sync.dma_start(out=out[b * P : (b + 1) * P, q0:q1], in_=res[b][:, q0:q1])

        for item in SEQ:
            if item[0] in "xabdogr":
                load("A0" if item == "a0" else item)
        la, lb, ld, pr, hb, si = {}, {}, {}, {}, {}, {}
        for item in SEQ:
            kind, i = item[0], int(item[1:])
            if kind == "x":
                tokens(i)
            elif kind == "a":
                la[i] = quantize_up(item, "w1", UP1[i])
            elif kind == "b":
                lb[i] = quantize_up(item, "w3", UP3[i])
                if i in MARKS:
                    nc.gpsimd.tensor_scalar(out=zeros[i][:], in0=lb[i][:, 0:1], scalar1=0.0, scalar2=0.0, op0=MULT, op1=ADD)
            elif kind == "d":
                ld[i] = lay_down(i)
            elif kind == "A":
                up1[i] = codes_up(la[i], "w1")
            elif kind == "B":
                up3[i] = codes_up(lb[i], "w3")
            elif kind == "D":
                dn[i] = codes_down(ld[i])
            elif kind == "G":
                gather(i)
            elif kind == "p":
                pr[i] = first_products(i)
            elif kind == "m":
                si[i] = silu_of(pr[i][0], i + 1)
            elif kind == "t":
                hb[i] = gated(pr[i][1], si[i])
            elif kind == "u":
                hid[i] = codes_hidden(hb[i])
            elif kind == "y":
                result(i)
            elif kind == "s":
                scatter(i)
